import numpy as np, ml_dtypes
CORES = [25,29,65,69,153,157,193,197]
N = 8
import mx_ref
NC, ROOT = 256, 5
BF = ml_dtypes.bfloat16
def cut(t, i, w=512):
    return t[:, w * i:w * i + w]
def term(a, B):
    return np.stack([np.maximum(mx_ref.matmul(mx_ref.quantize(cut(a, i)), B), 0) for i in range(4)], axis=2).reshape(128, -1)
def setup_inputs(rng):
    def f(*shape):
        return mx_ref.flush((rng.standard_normal(shape, dtype=np.float32) * np.exp2(rng.integers(-2, 3, shape[:-1] + (1,)))).astype(BF))
    return {"a": f(N, 128, 4 * 512), "b": f(N, 128, 4 * NC)}
def setup_inputs_blocks(rng):
    d = setup_inputs(rng)
    for k in ("a", "b"): d[k] = mx_ref.spread(d[k], rng, 2)
    return d
def setup_inputs_wide(rng):
    d = setup_inputs(rng)
    for k in ("a", "b"): d[k] = mx_ref.flush((d[k].astype(np.float32) * np.exp2(rng.integers(-4, 5, (N, 1, 1))).astype(np.float32)).astype(BF))
    return d
def setup_inputs_lossless(rng):
    a = np.zeros((N, 128, 4 * 128, 4), np.float32)
    for r in range(N):
        k = rng.integers(0, 512, size=4 * 128)
        a[r, k // 4, np.arange(4 * 128), k % 4] = 1.0
    size = np.repeat(2.0 ** rng.integers(-4, 5, size=(1, 1, (4 * NC) // 4)), 4, axis=2)
    b = (rng.random((N, 128, 4 * NC)) < 0.8) * size
    return {"a": a.reshape(N, 128, 4 * 512).astype(BF), "b": b.astype(np.float32).astype(BF)}
def reference(a, b):
    B0 = mx_ref.quantize(b[ROOT])
    T = [term(a[r], B0) for r in range(N)]
    y = np.zeros((N, 128, 4 * NC), np.float32)
    y[:] = mx_ref.total(T)
    return {"y": y}

@@ -1,0 +1,234 @@
+from concourse.bass import DstId, RemoteDMATransfer
+from concourse.mybir import dt, AluOpType, ActivationFunctionType
+
+WORLD = 256
+HALF = 128
+F8, U8, BF, F32 = "float8_e4m3fn_x4", "uint8", "bfloat16", "float32"
+
+SCRATCH = {
+    "bt": ("sbuf", [128, 1024], BF), "at": ("sbuf", [128, 2048], BF),
+    "bq": ("sbuf", [128, 256], F8), "bs": ("sbuf", [128, 256], U8),
+    "aq": ("sbuf", [128, 512], F8), "as": ("sbuf", [128, 512], U8),
+    "one": ("sbuf", [128, 128], BF), "sb": ("sbuf", [128, 512], BF),
+    "sq": ("sbuf", [128, 512], F8), "ss": ("sbuf", [128, 512], U8),
+    "tt": ("sbuf", [128, 1024], BF), "tq": ("sbuf", [128, 256], F8), "ts": ("sbuf", [128, 256], U8),
+    "lq": ("sbuf", [128, 512], F8), "ls": ("sbuf", [128, 512], U8),
+    "gt": ("sbuf", [128, 512], BF), "gq": ("sbuf", [128, 128], F8), "gs": ("sbuf", [128, 128], U8),
+    "oq": ("sbuf", [128, 256], F8), "os": ("sbuf", [128, 256], U8),
+    "cq": ("sbuf", [128, 256], F8), "cs": ("sbuf", [128, 256], U8),
+    "ys": ("sbuf", [128, 1024], F32),
+    "ps": ("psum", [128, 4096], F32),
+}
+SEMAPHORES = (["sent", "mk", "idt", "sqd", "cst", "lda", "ldb0", "ldb1", "qa", "qb0", "qb1", "b0", "b1", "ge", "gqd"]
+              + ["t%d" % s for s in range(4)] + ["gm%d" % b for b in range(4)]
+              + ["%s%d" % (n, h) for n in ("ev", "qt", "o", "c", "fe", "st") for h in range(2)]
+              + ["%s%d%d" % (n, h, i) for n in ("pm", "fm") for h in range(2) for i in range(4)])
+
+
+def ones(m):
+    return bin(m).count("1")
+
+
+def plan(T, topo):
+    home = lambda c: (topo.host(c), topo.chip(c))
+    root = T.cores[T.root]
+    ranks, cores = {}, {}
+    for c in T.cores:
+        ranks.setdefault(home(c), {})[topo.die(c)] = c
+    for c in range(WORLD):
+        cores.setdefault(home(c), []).append(c)
+    homes = list(ranks)
+    dies = sorted(ranks[homes[0]])
+    first = lambda m: ranks[m][dies[0]]
+    peer = {m: [k for k in homes if topo.same_plane(first(m), first(k))][0] for m in homes}
+    far = {m: [k for k in homes if k not in (m, peer[m])] for m in homes}
+    cross = {m: [k for k in far[m] if k[0] == m[0]][0] for m in homes}
+    ports = {m: {d: [c for c in cores[m] if topo.die(c) == d and topo.may_write(c, first(cross[m]))] for d in dies} for m in homes}
+    adder = {m: [ports[m][d][0] for d in dies] for m in homes}
+    off = {c: topo.mask(c, first(peer[m])) for m in homes for c in cores[m]}
+    on = {c: topo.mask(c, [k for k in cores[m] if k != c][0]) for m in homes for c in cores[m]}
+    near = {c: on[c] & ~off[c] for c in on}
+    steps, made = {c: [] for c in range(WORLD)}, {}
+
+    R = home(root)
+    relay = {h: {d: ports[R][d][h] for d in dies} for h in range(2)}
+    for m in homes:
+        own = [ranks[m][d] for d in dies]
+        users = own + adder[m]
+        makers = [[(c, 0, HALF)] for c in users]
+        if m == R:
+            mate = [c for c in own if c != root][0]
+            x, y = [relay[1][d] for d in dies]
+            u, v = adder[m]
+            makers = [[(x, 0, HALF)], [(y, 0, HALF)], [(u, 0, HALF // 2), (v, HALF // 2, HALF)], [(root, 0, HALF // 4), (mate, HALF // 4, HALF)]]
+        for b, ms in enumerate(makers):
+            to = [u for u in users if u not in [c for c, _, _ in ms]]
+            for c, lo, hi in ms:
+                made[c] = b
+                mask = on[c] if c in users else off[c]
+                steps[c].append(("sqd", 1, [("sq", "ss", HALF * b + lo, hi - lo, to, "sq", "ss", HALF * b + lo, mask, "cst")]))
+    def bit(h, to, mask):
+        return ("bq", "bs", HALF * h, HALF, to, "bq", "bs", HALF * h, mask, "b%d" % h)
+    for h in range(2):
+        steps[root].append(("qb%d" % h, 1, [bit(h, [relay[h][d] for d in dies], on[root])]))
+        for d in dies:
+            c = relay[h][d]
+            steps[c].append(("b%d" % h, None, [bit(h, [ranks[k][d] for k in far[R]], off[c])]))
+    for d in dies:
+        c, to = ranks[R][d], ranks[peer[R]][d]
+        more = [bit(0, [to], off[relay[0][d]])]
+        if c != root:
+            more.append(bit(0, [c], near[relay[0][d]]))
+            steps[c].append(("b1", None, [bit(1, [to], off[c])]))
+        else:
+            steps[c].append(("qb1", 1, [bit(1, [to], off[c])] + [bit(1, [k], near[c]) for k in ranks[R].values() if k != c]))
+        steps[relay[0][d]].append(("b0", None, more))
+    src = {}
+    for m in homes:
+        for c in ranks[m].values():
+            n = len([k for k in T.cores if k < c and (home(k) == m or home(k) == peer[m])])
+            src[c] = n
+            for h in range(2):
+                steps[c].append(("qt%d" % h, 1, [("tq", "ts", HALF * h, HALF, [adder[k][h]], "lq", "ls", HALF * n, mask, "t%d" % n)
+                                                for k, mask in ((peer[m], off[c]), (m, near[c]))]))
+    for m in homes:
+        for h in range(2):
+            c = adder[m][h]
+            steps[c].append(("gqd", 1, [("gq", "gs", 0, HALF, list(ranks[cross[m]].values()), "cq", "cs", HALF * h, off[c], "c%d" % h),
+                                        ("gq", "gs", 0, HALF, list(ranks[m].values()), "oq", "os", HALF * h, near[c], "o%d" % h)]))
+    arrive = {}
+    for c in range(WORLD):
+        for _, _, items in steps[c]:
+            for it in items:
+                for k in it[4]:
+                    arrive[(k, it[9])] = arrive.get((k, it[9]), 0) + 2 * ones(it[8])
+    order = {}
+    for m in homes:
+        mine = [c for k in (m, peer[m]) for c in ranks[k].values()]
+        for c in adder[m]:
+            order[c] = [src[k] for k in sorted(mine, key=lambda k: (home(k) != R, k != root, home(k) != m, k))]
+    return steps, arrive, made, order
+
+
+def rank_program(g, core, T, topo):
+    steps, arrive, made, order = plan(T, topo)
+    rank = T.rank_of(core)
+    if not steps[core]:
+        return
+    sem = lambda name: T.sem[name]
+    root = rank is not None and rank == T.root
+    adds = core in order
+    V, S, P, Y = g.vector, g.scalar, g.tensor, g.sync
+
+    if root:
+        Y.dma_start(T.bt[:, 0:512], T.b[:, 0:512]).then_inc(sem("ldb0"), 16)
+        S.dma_start(T.bt[:, 512:1024], T.b[:, 512:1024]).then_inc(sem("ldb1"), 16)
+    if rank is not None:
+        Y.dma_start(T.at[:], T.a[:]).then_inc(sem("lda"), 16)
+
+    k = made[core]
+    V.memset(T.one[:], 1.0).then_inc(sem("mk"), 1)
+    V.memset(T.sb[:], 0.0).then_inc(sem("mk"), 1)
+    g.wait_ge(sem("mk"), 2)
+    g.affine_select(T.sb[:, k:512:4], T.one[:], [[-1, 128]], AluOpType.is_equal, 0.0, 0, 1).then_inc(sem("idt"), 1)
+    V.wait_ge(sem("idt"), 1)
+    V.quantize_mx(T.sq[:, HALF * k:HALF * k + HALF], T.ss[:, HALF * k:HALF * k + HALF], T.sb[:]).then_inc(sem("sqd"), 1)
+
+    sent = [0]
+    for name, count, items in steps[core]:
+        g.wait_ge(sem(name), arrive[(core, name)] if count is None else count)
+        for part in range(2):
+            transfers = []
+            for it in items:
+                a, n, there, z, mask = it[2], it[3], it[4], it[7], it[8]
+                x, y = T[it[part]][:, a:a + n], T[it[5 + part]][:, z:z + n]
+                ids = []
+                for d in there:
+                    rid, pid = topo.addr(d, core)
+                    ids.append(DstId(rid=rid, pnc=pid))
+                if part == 0:
+                    x, y = x.bitcast(dt.uint8), y.bitcast(dt.uint8)
+                transfers.append(RemoteDMATransfer(dst_ids=ids, dma_engine_mask=mask, remote_sem=sem(it[9]), srcs=[x], dsts=[y for _ in there]))
+                sent[0] += ones(mask)
+            g.remote_dma_fused(transfers, local_sem=sem("sent"))
+    g.wait_ge(sem("sent"), sent[0])
+
+    def bank(j, n=HALF):
+        return T.ps[:, 512 * j:512 * j + n]
+
+    def unpack(j, b, q, s, c, start, stop):
+        return P.matmul_mx(bank(j), T.sq[:, HALF * b:HALF * b + HALF], T.ss[:, HALF * b:HALF * b + HALF],
+                           T[q][:, c:c + HALF], T[s][:, c:c + HALF], start, stop)
+
+    if adds:
+        P.wait_ge(sem("sqd"), 1)
+        P.wait_ge(sem("cst"), arrive[(core, "cst")])
+        for pos, s in enumerate(order[core]):
+            P.wait_ge(sem("t%d" % s), arrive[(core, "t%d" % s)])
+            for b in range(4):
+                m = unpack(b, b, "lq", "ls", HALF * s, pos == 0, pos == 3)
+                if pos == 3:
+                    m.then_inc(sem("gm%d" % b), 1)
+        for b in range(4):
+            if b % 2:
+                V.wait_ge(sem("gm%d" % b), 1)
+                V.tensor_copy(T.gt[:, b:512:4], bank(b)).then_inc(sem("ge"), 1)
+            else:
+                S.wait_ge(sem("gm%d" % b), 1)
+                S.activation(T.gt[:, b:512:4], bank(b), ActivationFunctionType.Copy).then_inc(sem("ge"), 1)
+        V.wait_ge(sem("ge"), 4)
+        V.quantize_mx(T.gq[:], T.gs[:], T.gt[:]).then_inc(sem("gqd"), 1)
+
+    if rank is None:
+        return
+
+    if root:
+        for h in range(2):
+            V.wait_ge(sem("ldb%d" % h), 16)
+            V.quantize_mx(T.bq[:, HALF * h:HALF * h + HALF], T.bs[:, HALF * h:HALF * h + HALF], T.bt[:, 512 * h:512 * h + 512]).then_inc(sem("qb%d" % h), 1)
+    V.wait_ge(sem("lda"), 16)
+    for i in range(4):
+        V.quantize_mx(T.aq[:, HALF * i:HALF * i + HALF], T["as"][:, HALF * i:HALF * i + HALF], T.at[:, 512 * i:512 * i + 512]).then_inc(sem("qa"), 1)
+
+    P.wait_ge(sem("qa"), 4)
+    for h in range(2):
+        if root:
+            P.wait_ge(sem("qb%d" % h), 1)
+        else:
+            P.wait_ge(sem("b%d" % h), arrive[(core, "b%d" % h)])
+        for i in range(4):
+            P.matmul_mx(bank(4 * h + i), T.aq[:, HALF * i:HALF * i + HALF], T["as"][:, HALF * i:HALF * i + HALF],
+                        T.bq[:, HALF * h:HALF * h + HALF], T.bs[:, HALF * h:HALF * h + HALF], True, True).then_inc(sem("pm%d%d" % (h, i)), 1)
+        for i in range(4):
+            out = T.tt[:, 512 * h + i:512 * h + 512:4]
+            q = V if i % 2 else S
+            q.wait_ge(sem("pm%d%d" % (h, i)), 1)
+            if i % 2:
+                V.tensor_scalar(out, bank(4 * h + i), 0.0, None, AluOpType.max).then_inc(sem("ev%d" % h), 1)
+            else:
+                S.activation(out, bank(4 * h + i), ActivationFunctionType.Relu).then_inc(sem("ev%d" % h), 1)
+        V.wait_ge(sem("ev%d" % h), 4)
+        V.quantize_mx(T.tq[:, HALF * h:HALF * h + HALF], T.ts[:, HALF * h:HALF * h + HALF], T.tt[:, 512 * h:512 * h + 512]).then_inc(sem("qt%d" % h), 1)
+
+    P.wait_ge(sem("sqd"), 1)
+    P.wait_ge(sem("cst"), arrive[(core, "cst")])
+    for h in range(2):
+        P.wait_ge(sem("ev%d" % h), 4)
+        P.wait_ge(sem("o%d" % h), arrive[(core, "o%d" % h)])
+        for b in range(4):
+            unpack(4 * h + b, b, "oq", "os", HALF * h, True, False)
+        P.wait_ge(sem("c%d" % h), arrive[(core, "c%d" % h)])
+        for b in range(4):
+            unpack(4 * h + b, b, "cq", "cs", HALF * h, False, True).then_inc(sem("fm%d%d" % (h, b)), 1)
+        for b in range(4):
+            out = T.ys[:, 512 * h + b:512 * h + 512:4]
+            q = V if b % 2 else S
+            q.wait_ge(sem("fm%d%d" % (h, b)), 1)
+            if b % 2:
+                V.tensor_copy(out, bank(4 * h + b)).then_inc(sem("fe%d" % h), 1)
+            else:
+                S.activation(out, bank(4 * h + b), ActivationFunctionType.Copy).then_inc(sem("fe%d" % h), 1)
+        Y.wait_ge(sem("fe%d" % h), 4)
+        Y.dma_start(T.y[:, 512 * h:512 * h + 512], T.ys[:, 512 * h:512 * h + 512]).then_inc(sem("st%d" % h), 16)
+    for h in range(2):
+        Y.wait_ge(sem("st%d" % h), 16)

@@ -9,20 +9,22 @@ SCRATCH = {
     "bt": ("sbuf", [128, 1024], BF), "at": ("sbuf", [128, 2048], BF),
     "bq": ("sbuf", [128, 256], F8), "bs": ("sbuf", [128, 256], U8),
     "aq": ("sbuf", [128, 512], F8), "as": ("sbuf", [128, 512], U8),
-    "one": ("sbuf", [128, 128], BF), "sb": ("sbuf", [128, 512], BF),
+    "one": ("sbuf", [128, 128], BF), "sb": ("sbuf", [128, 1536], BF),
     "sq": ("sbuf", [128, 512], F8), "ss": ("sbuf", [128, 512], U8),
-    "tt": ("sbuf", [128, 1024], BF), "tq": ("sbuf", [128, 256], F8), "ts": ("sbuf", [128, 256], U8),
-    "lq": ("sbuf", [128, 512], F8), "ls": ("sbuf", [128, 512], U8),
+    "wq": ("sbuf", [128, 1024], F8), "ws": ("sbuf", [128, 1024], U8),
+    "x0": ("sbuf", [128, 512], BF), "x1": ("sbuf", [128, 512], BF),
     "gt": ("sbuf", [128, 512], BF), "gq": ("sbuf", [128, 128], F8), "gs": ("sbuf", [128, 128], U8),
-    "oq": ("sbuf", [128, 256], F8), "os": ("sbuf", [128, 256], U8),
-    "cq": ("sbuf", [128, 256], F8), "cs": ("sbuf", [128, 256], U8),
+    "lq": ("sbuf", [128, 256], F8), "ls": ("sbuf", [128, 256], U8),
+    "cq": ("sbuf", [128, 512], F8), "cs": ("sbuf", [128, 512], U8),
     "ys": ("sbuf", [128, 1024], F32),
     "ps": ("psum", [128, 4096], F32),
 }
-SEMAPHORES = (["sent", "mk", "idt", "sqd", "cst", "lda", "ldb0", "ldb1", "qa", "qb0", "qb1", "b0", "b1", "ge", "gqd"]
-              + ["t%d" % s for s in range(4)] + ["gm%d" % b for b in range(4)]
-              + ["%s%d" % (n, h) for n in ("ev", "qt", "o", "c", "fe", "st") for h in range(2)]
-              + ["%s%d%d" % (n, h, i) for n in ("pm", "fm") for h in range(2) for i in range(4)])
+SEMAPHORES = (["sent", "mk", "idt", "sqd", "cst", "lda", "qa", "w0", "w1", "qb0", "qb1", "ldb0", "ldb1", "bc", "bp", "t0", "t1", "gqd", "dn"]
+              + ["%s%d" % (n, i) for n in ("x", "gm") for i in range(4)]
+              + ["pm%d%d" % (s, i) for s in range(2) for i in range(4)]
+              + ["c%d%d" % (k, h) for k in range(2) for h in range(2)]
+              + ["%s%d" % (n, h) for n in ("fe", "st") for h in range(2)]
+              + ["fm%d%d" % (h, i) for h in range(2) for i in range(4)])
 
 
 def ones(m):
@@ -40,85 +42,83 @@ def plan(T, topo):
     homes = list(ranks)
     dies = sorted(ranks[homes[0]])
     first = lambda m: ranks[m][dies[0]]
+    R = home(root)
     peer = {m: [k for k in homes if topo.same_plane(first(m), first(k))][0] for m in homes}
-    far = {m: [k for k in homes if k not in (m, peer[m])] for m in homes}
-    cross = {m: [k for k in far[m] if k[0] == m[0]][0] for m in homes}
-    ports = {m: {d: [c for c in cores[m] if topo.die(c) == d and topo.may_write(c, first(cross[m]))] for d in dies} for m in homes}
-    adder = {m: [ports[m][d][0] for d in dies] for m in homes}
+    far = {m: sorted([k for k in homes if k not in (m, peer[m])], key=lambda k: k[0] != m[0]) for m in homes}
+    ports = {m: {d: [c for c in cores[m] if topo.die(c) == d and topo.may_write(c, first(far[m][0]))] for d in dies} for m in homes}
+    W = {m: [ports[m][d][0] for d in dies] for m in homes}
+    H = {m: [ports[m][d][1] for d in dies] for m in homes}
     off = {c: topo.mask(c, first(peer[m])) for m in homes for c in cores[m]}
     on = {c: topo.mask(c, [k for k in cores[m] if k != c][0]) for m in homes for c in cores[m]}
     near = {c: on[c] & ~off[c] for c in on}
     steps, made = {c: [] for c in range(WORLD)}, {}
 
-    R = home(root)
-    relay = {h: {d: ports[R][d][h] for d in dies} for h in range(2)}
+    def call(c, wait, *tr):
+        steps[c].append((wait, list(tr)))
+
+    for m in homes:
+        p, q = [ranks[m][d] for d in dies]
+        made[p], made[q], made[W[m][0]], made[W[m][1]] = [0], [1], [0], [1]
+        made[H[m][0]], made[H[m][1]] = [2, 0, 1], [3, 0, 1]
+        for c, b, lo, hi, to in [(p, 0, 0, 32, [q]), (q, 1, 0, 32, [p]), (W[m][0], 0, 32, HALF, [q]), (W[m][1], 1, 32, HALF, [p]),
+                                 (H[m][0], 2, 0, HALF, [H[m][1], p, q]), (H[m][1], 3, 0, HALF, [H[m][0], p, q])]:
+            for t in ("sq", "ss"):
+                call(c, ("sqd", 1), (t, HALF * b + lo, hi - lo, t, to, HALF * b + lo, on[c], "cst"))
+    for h in range(2):
+        w, r, z = W[R][h], H[R][h], HALF * h
+        to = [W[k][h] for k in far[R]] + [W[peer[R]][h]]
+        call(root, ("qb%d" % h, 1), ("bq", z, HALF, "bq", [w], z, on[root], "bc"))
+        call(root, ("qb%d" % h, 1), ("bs", z, HALF, "bs", [r], z, on[root], "bp"))
+        call(w, ("bc", None), ("bq", z, HALF, "bq", to, z, off[w], "bc"))
+        call(r, ("bp", None), ("bs", z, HALF, "bs", to, z, off[r], "bp"))
+    for h in range(2):
+        z = HALF * h
+        call(root, ("qb%d" % h, 1), ("bs", z, HALF, "bs", [W[R][h]], z, on[root], "bp"))
+    for m in homes:
+        for s, d in enumerate(dies):
+            c = ranks[m][d]
+            for t in "qs":
+                call(c, ("qa", 4), ("a" + t, 0, 512, "w" + t, W[m], 512 * s, on[c], "w%d" % s))
     for m in homes:
         own = [ranks[m][d] for d in dies]
-        users = own + adder[m]
-        makers = [[(c, 0, HALF)] for c in users]
-        if m == R:
-            mate = [c for c in own if c != root][0]
-            x, y = [relay[1][d] for d in dies]
-            u, v = adder[m]
-            makers = [[(x, 0, HALF)], [(y, 0, HALF)], [(u, 0, HALF // 2), (v, HALF // 2, HALF)], [(root, 0, HALF // 4), (mate, HALF // 4, HALF)]]
-        for b, ms in enumerate(makers):
-            to = [u for u in users if u not in [c for c, _, _ in ms]]
-            for c, lo, hi in ms:
-                made[c] = b
-                mask = on[c] if c in users else off[c]
-                steps[c].append(("sqd", 1, [("sq", "ss", HALF * b + lo, hi - lo, to, "sq", "ss", HALF * b + lo, mask, "cst")]))
-    def bit(h, to, mask):
-        return ("bq", "bs", HALF * h, HALF, to, "bq", "bs", HALF * h, mask, "b%d" % h)
-    for h in range(2):
-        steps[root].append(("qb%d" % h, 1, [bit(h, [relay[h][d] for d in dies], on[root])]))
-        for d in dies:
-            c = relay[h][d]
-            steps[c].append(("b%d" % h, None, [bit(h, [ranks[k][d] for k in far[R]], off[c])]))
-    for d in dies:
-        c, to = ranks[R][d], ranks[peer[R]][d]
-        more = [bit(0, [to], off[relay[0][d]])]
-        if c != root:
-            more.append(bit(0, [c], near[relay[0][d]]))
-            steps[c].append(("b1", None, [bit(1, [to], off[c])]))
-        else:
-            steps[c].append(("qb1", 1, [bit(1, [to], off[c])] + [bit(1, [k], near[c]) for k in ranks[R].values() if k != c]))
-        steps[relay[0][d]].append(("b0", None, more))
-    src = {}
-    for m in homes:
-        for c in ranks[m].values():
-            n = len([k for k in T.cores if k < c and (home(k) == m or home(k) == peer[m])])
-            src[c] = n
-            for h in range(2):
-                steps[c].append(("qt%d" % h, 1, [("tq", "ts", HALF * h, HALF, [adder[k][h]], "lq", "ls", HALF * n, mask, "t%d" % n)
-                                                for k, mask in ((peer[m], off[c]), (m, near[c]))]))
-    for m in homes:
+        cross = [ranks[far[m][0]][d] for d in dies]
         for h in range(2):
-            c = adder[m][h]
-            steps[c].append(("gqd", 1, [("gq", "gs", 0, HALF, list(ranks[cross[m]].values()), "cq", "cs", HALF * h, off[c], "c%d" % h),
-                                        ("gq", "gs", 0, HALF, list(ranks[m].values()), "oq", "os", HALF * h, near[c], "o%d" % h)]))
+            w, r = W[m][h], H[m][h]
+            for t in "qs":
+                call(w, ("gqd", 1), ("g" + t, 0, HALF, "l" + t, [H[peer[m]][h]], HALF, off[w], "t1"),
+                     ("g" + t, 0, HALF, "l" + t, [r], 0, near[w], "t0"))
+            for t in "qs":
+                call(r, ("gqd", 1), ("g" + t, 0, HALF, "c" + t, cross, 256 + HALF * h, off[r], "c1%d" % h),
+                     ("g" + t, 0, HALF, "c" + t, own, HALF * h, near[r], "c0%d" % h))
     arrive = {}
     for c in range(WORLD):
-        for _, _, items in steps[c]:
-            for it in items:
-                for k in it[4]:
-                    arrive[(k, it[9])] = arrive.get((k, it[9]), 0) + 2 * ones(it[8])
-    order = {}
-    for m in homes:
-        mine = [c for k in (m, peer[m]) for c in ranks[k].values()]
-        for c in adder[m]:
-            order[c] = [src[k] for k in sorted(mine, key=lambda k: (home(k) != R, k != root, home(k) != m, k))]
-    return steps, arrive, made, order
+        for _, tr in steps[c]:
+            for t in tr:
+                for k in t[4]:
+                    arrive[(k, t[7])] = arrive.get((k, t[7]), 0) + ones(t[6])
+    work = {c: h for m in homes for h, c in enumerate(W[m])}
+    adds = [c for m in homes for c in H[m]]
+    return steps, arrive, made, work, adds
 
 
 def rank_program(g, core, T, topo):
-    steps, arrive, made, order = plan(T, topo)
+    steps, arrive, made, work, adds = plan(T, topo)
     rank = T.rank_of(core)
     if not steps[core]:
         return
     sem = lambda name: T.sem[name]
     root = rank is not None and rank == T.root
-    adds = core in order
     V, S, P, Y = g.vector, g.scalar, g.tensor, g.sync
+
+    def arr(q, name):
+        q.wait_ge(sem(name), arrive[(core, name)])
+
+    def bank(j):
+        return T.ps[:, 512 * j:512 * j + HALF]
+
+    def unpack(j, b, q, s, z, start, stop):
+        return P.matmul_mx(bank(j), T.sq[:, HALF * b:HALF * b + HALF], T.ss[:, HALF * b:HALF * b + HALF],
+                           T[q][:, z:z + HALF], T[s][:, z:z + HALF], start, stop)
 
     if root:
         Y.dma_start(T.bt[:, 0:512], T.b[:, 0:512]).then_inc(sem("ldb0"), 16)
@@ -126,59 +126,73 @@ def rank_program(g, core, T, topo):
     if rank is not None:
         Y.dma_start(T.at[:], T.a[:]).then_inc(sem("lda"), 16)
 
-    k = made[core]
+    mine = made[core]
     V.memset(T.one[:], 1.0).then_inc(sem("mk"), 1)
-    V.memset(T.sb[:], 0.0).then_inc(sem("mk"), 1)
+    V.memset(T.sb[:, 0:512 * len(mine)], 0.0).then_inc(sem("mk"), 1)
     g.wait_ge(sem("mk"), 2)
-    g.affine_select(T.sb[:, k:512:4], T.one[:], [[-1, 128]], AluOpType.is_equal, 0.0, 0, 1).then_inc(sem("idt"), 1)
-    V.wait_ge(sem("idt"), 1)
-    V.quantize_mx(T.sq[:, HALF * k:HALF * k + HALF], T.ss[:, HALF * k:HALF * k + HALF], T.sb[:]).then_inc(sem("sqd"), 1)
+    for j, b in enumerate(mine):
+        g.affine_select(T.sb[:, 512 * j + b:512 * j + 512:4], T.one[:], [[-1, 128]], AluOpType.is_equal, 0.0, 0, 1).then_inc(sem("idt"), 1)
+    for j, b in enumerate(mine):
+        V.wait_ge(sem("idt"), j + 1)
+        V.quantize_mx(T.sq[:, HALF * b:HALF * b + HALF], T.ss[:, HALF * b:HALF * b + HALF], T.sb[:, 512 * j:512 * j + 512]).then_inc(sem("sqd"), 1)
 
-    sent = [0]
-    for name, count, items in steps[core]:
+    sent = 0
+    for (name, count), tr in steps[core]:
         g.wait_ge(sem(name), arrive[(core, name)] if count is None else count)
-        for part in range(2):
-            transfers = []
-            for it in items:
-                a, n, there, z, mask = it[2], it[3], it[4], it[7], it[8]
-                x, y = T[it[part]][:, a:a + n], T[it[5 + part]][:, z:z + n]
-                ids = []
-                for d in there:
-                    rid, pid = topo.addr(d, core)
-                    ids.append(DstId(rid=rid, pnc=pid))
-                if part == 0:
-                    x, y = x.bitcast(dt.uint8), y.bitcast(dt.uint8)
-                transfers.append(RemoteDMATransfer(dst_ids=ids, dma_engine_mask=mask, remote_sem=sem(it[9]), srcs=[x], dsts=[y for _ in there]))
-                sent[0] += ones(mask)
-            g.remote_dma_fused(transfers, local_sem=sem("sent"))
-    g.wait_ge(sem("sent"), sent[0])
+        ts = []
+        for a, z0, n, b, to, z1, mask, s in tr:
+            x, y = T[a][:, z0:z0 + n], T[b][:, z1:z1 + n]
+            if a[-1] == "q":
+                x, y = x.bitcast(dt.uint8), y.bitcast(dt.uint8)
+            ids = []
+            for d in to:
+                rid, pid = topo.addr(d, core)
+                ids.append(DstId(rid=rid, pnc=pid))
+            ts.append(RemoteDMATransfer(dst_ids=ids, dma_engine_mask=mask, remote_sem=sem(s), srcs=[x], dsts=[y for _ in to]))
+            sent += ones(mask)
+        g.remote_dma_fused(ts, local_sem=sem("sent"))
+    g.wait_ge(sem("sent"), sent)
 
-    def bank(j, n=HALF):
-        return T.ps[:, 512 * j:512 * j + n]
+    if core in work:
+        z = HALF * work[core]
+        for name in ("bc", "bp", "w0", "w1"):
+            arr(P, name)
+        for i in range(4):
+            for s in range(2):
+                c = 512 * s + HALF * i
+                P.matmul_mx(bank(4 * s + i), T.wq[:, c:c + HALF], T.ws[:, c:c + HALF],
+                            T.bq[:, z:z + HALF], T.bs[:, z:z + HALF], True, True).then_inc(sem("pm%d%d" % (s, i)), 1)
+        for i in range(4):
+            for s in range(2):
+                out = (T.x0, T.x1)[s][:, i:512:4]
+                onv = (s, i) == (1, 0)
+                (V if onv else S).wait_ge(sem("pm%d%d" % (s, i)), 1)
+                if onv:
+                    V.tensor_scalar(out, bank(4 * s + i), 0.0, None, AluOpType.max).then_inc(sem("x%d" % i), 1)
+                else:
+                    S.activation(out, bank(4 * s + i), ActivationFunctionType.Relu).then_inc(sem("x%d" % i), 1)
+            V.wait_ge(sem("x%d" % i), 2)
+            V.tensor_tensor(T.gt[:, i:512:4], T.x0[:, i:512:4], T.x1[:, i:512:4], AluOpType.add).then_inc(sem("dn"), 1)
 
-    def unpack(j, b, q, s, c, start, stop):
-        return P.matmul_mx(bank(j), T.sq[:, HALF * b:HALF * b + HALF], T.ss[:, HALF * b:HALF * b + HALF],
-                           T[q][:, c:c + HALF], T[s][:, c:c + HALF], start, stop)
-
-    if adds:
-        P.wait_ge(sem("sqd"), 1)
-        P.wait_ge(sem("cst"), arrive[(core, "cst")])
-        for pos, s in enumerate(order[core]):
-            P.wait_ge(sem("t%d" % s), arrive[(core, "t%d" % s)])
+    if core in adds:
+        P.wait_ge(sem("sqd"), len(mine))
+        arr(P, "cst")
+        for s in range(2):
+            arr(P, "t%d" % s)
             for b in range(4):
-                m = unpack(b, b, "lq", "ls", HALF * s, pos == 0, pos == 3)
-                if pos == 3:
-                    m.then_inc(sem("gm%d" % b), 1)
+                mm = unpack(b, b, "lq", "ls", HALF * s, s == 0, s == 1)
+                if s == 1:
+                    mm.then_inc(sem("gm%d" % b), 1)
         for b in range(4):
             if b % 2:
                 V.wait_ge(sem("gm%d" % b), 1)
-                V.tensor_copy(T.gt[:, b:512:4], bank(b)).then_inc(sem("ge"), 1)
+                V.tensor_copy(T.gt[:, b:512:4], bank(b)).then_inc(sem("dn"), 1)
             else:
                 S.wait_ge(sem("gm%d" % b), 1)
-                S.activation(T.gt[:, b:512:4], bank(b), ActivationFunctionType.Copy).then_inc(sem("ge"), 1)
-        V.wait_ge(sem("ge"), 4)
+                S.activation(T.gt[:, b:512:4], bank(b), ActivationFunctionType.Copy).then_inc(sem("dn"), 1)
+    if core in work or core in adds:
+        V.wait_ge(sem("dn"), 4)
         V.quantize_mx(T.gq[:], T.gs[:], T.gt[:]).then_inc(sem("gqd"), 1)
-
     if rank is None:
         return
 
@@ -190,43 +204,23 @@ def rank_program(g, core, T, topo):
     for i in range(4):
         V.quantize_mx(T.aq[:, HALF * i:HALF * i + HALF], T["as"][:, HALF * i:HALF * i + HALF], T.at[:, 512 * i:512 * i + 512]).then_inc(sem("qa"), 1)
 
-    P.wait_ge(sem("qa"), 4)
+    P.wait_ge(sem("sqd"), len(mine))
+    arr(P, "cst")
+    for k in range(2):
+        for h in range(2):
+            arr(P, "c%d%d" % (k, h))
+            for b in range(4):
+                mm = unpack(4 * h + b, b, "cq", "cs", 256 * k + HALF * h, k == 0, k == 1)
+                if k == 1:
+                    mm.then_inc(sem("fm%d%d" % (h, b)), 1)
     for h in range(2):
-        if root:
-            P.wait_ge(sem("qb%d" % h), 1)
-        else:
-            P.wait_ge(sem("b%d" % h), arrive[(core, "b%d" % h)])
-        for i in range(4):
-            P.matmul_mx(bank(4 * h + i), T.aq[:, HALF * i:HALF * i + HALF], T["as"][:, HALF * i:HALF * i + HALF],
-                        T.bq[:, HALF * h:HALF * h + HALF], T.bs[:, HALF * h:HALF * h + HALF], True, True).then_inc(sem("pm%d%d" % (h, i)), 1)
-        for i in range(4):
-            out = T.tt[:, 512 * h + i:512 * h + 512:4]
-            q = V if i % 2 else S
-            q.wait_ge(sem("pm%d%d" % (h, i)), 1)
-            if i % 2:
-                V.tensor_scalar(out, bank(4 * h + i), 0.0, None, AluOpType.max).then_inc(sem("ev%d" % h), 1)
-            else:
-                S.activation(out, bank(4 * h + i), ActivationFunctionType.Relu).then_inc(sem("ev%d" % h), 1)
-        V.wait_ge(sem("ev%d" % h), 4)
-        V.quantize_mx(T.tq[:, HALF * h:HALF * h + HALF], T.ts[:, HALF * h:HALF * h + HALF], T.tt[:, 512 * h:512 * h + 512]).then_inc(sem("qt%d" % h), 1)
-
-    P.wait_ge(sem("sqd"), 1)
-    P.wait_ge(sem("cst"), arrive[(core, "cst")])
-    for h in range(2):
-        P.wait_ge(sem("ev%d" % h), 4)
-        P.wait_ge(sem("o%d" % h), arrive[(core, "o%d" % h)])
-        for b in range(4):
-            unpack(4 * h + b, b, "oq", "os", HALF * h, True, False)
-        P.wait_ge(sem("c%d" % h), arrive[(core, "c%d" % h)])
-        for b in range(4):
-            unpack(4 * h + b, b, "cq", "cs", HALF * h, False, True).then_inc(sem("fm%d%d" % (h, b)), 1)
         for b in range(4):
             out = T.ys[:, 512 * h + b:512 * h + 512:4]
-            q = V if b % 2 else S
-            q.wait_ge(sem("fm%d%d" % (h, b)), 1)
             if b % 2:
+                V.wait_ge(sem("fm%d%d" % (h, b)), 1)
                 V.tensor_copy(out, bank(4 * h + b)).then_inc(sem("fe%d" % h), 1)
             else:
+                S.wait_ge(sem("fm%d%d" % (h, b)), 1)
                 S.activation(out, bank(4 * h + b), ActivationFunctionType.Copy).then_inc(sem("fe%d" % h), 1)
         Y.wait_ge(sem("fe%d" % h), 4)
         Y.dma_start(T.y[:, 512 * h:512 * h + 512], T.ys[:, 512 * h:512 * h + 512]).then_inc(sem("st%d" % h), 16)

from concourse.bass import DstId, RemoteDMATransfer
from concourse.mybir import dt, AluOpType, ActivationFunctionType

WORLD = 256
HALF = 128
F8, U8, BF, F32 = "float8_e4m3fn_x4", "uint8", "bfloat16", "float32"

SCRATCH = {
    "bt": ("sbuf", [128, 1024], BF), "at": ("sbuf", [128, 2048], BF),
    "bq": ("sbuf", [128, 256], F8), "bs": ("sbuf", [128, 256], U8),
    "aq": ("sbuf", [128, 512], F8), "as": ("sbuf", [128, 512], U8),
    "one": ("sbuf", [128, 128], BF), "sb": ("sbuf", [128, 1536], BF),
    "sq": ("sbuf", [128, 512], F8), "ss": ("sbuf", [128, 512], U8),
    "wq": ("sbuf", [128, 1024], F8), "ws": ("sbuf", [128, 1024], U8),
    "x0": ("sbuf", [128, 512], BF), "x1": ("sbuf", [128, 512], BF),
    "gt": ("sbuf", [128, 512], BF), "gq": ("sbuf", [128, 128], F8), "gs": ("sbuf", [128, 128], U8),
    "lq": ("sbuf", [128, 256], F8), "ls": ("sbuf", [128, 256], U8),
    "cq": ("sbuf", [128, 512], F8), "cs": ("sbuf", [128, 512], U8),
    "ys": ("sbuf", [128, 1024], F32),
    "ps": ("psum", [128, 4096], F32),
}
SEMAPHORES = (["sent", "mk", "idt", "sqd", "cst", "lda", "qa", "w0", "w1", "qb0", "qb1", "ldb0", "ldb1", "bc", "bp", "t0", "t1", "gqd", "dn"]
              + ["%s%d" % (n, i) for n in ("x", "gm") for i in range(4)]
              + ["pm%d%d" % (s, i) for s in range(2) for i in range(4)]
              + ["c%d%d" % (k, h) for k in range(2) for h in range(2)]
              + ["%s%d" % (n, h) for n in ("fe", "st") for h in range(2)]
              + ["fm%d%d" % (h, i) for h in range(2) for i in range(4)])


def ones(m):
    return bin(m).count("1")


def plan(T, topo):
    home = lambda c: (topo.host(c), topo.chip(c))
    root = T.cores[T.root]
    ranks, cores = {}, {}
    for c in T.cores:
        ranks.setdefault(home(c), {})[topo.die(c)] = c
    for c in range(WORLD):
        cores.setdefault(home(c), []).append(c)
    homes = list(ranks)
    dies = sorted(ranks[homes[0]])
    first = lambda m: ranks[m][dies[0]]
    R = home(root)
    peer = {m: [k for k in homes if topo.same_plane(first(m), first(k))][0] for m in homes}
    far = {m: sorted([k for k in homes if k not in (m, peer[m])], key=lambda k: k[0] != m[0]) for m in homes}
    ports = {m: {d: [c for c in cores[m] if topo.die(c) == d and topo.may_write(c, first(far[m][0]))] for d in dies} for m in homes}
    W = {m: [ports[m][d][0] for d in dies] for m in homes}
    H = {m: [ports[m][d][1] for d in dies] for m in homes}
    off = {c: topo.mask(c, first(peer[m])) for m in homes for c in cores[m]}
    on = {c: topo.mask(c, [k for k in cores[m] if k != c][0]) for m in homes for c in cores[m]}
    near = {c: on[c] & ~off[c] for c in on}
    steps, made = {c: [] for c in range(WORLD)}, {}

    def call(c, wait, *tr):
        steps[c].append((wait, list(tr)))

    for m in homes:
        p, q = [ranks[m][d] for d in dies]
        made[p], made[q], made[W[m][0]], made[W[m][1]] = [0], [1], [0], [1]
        made[H[m][0]], made[H[m][1]] = [2, 0, 1], [3, 0, 1]
        for c, b, lo, hi, to in [(p, 0, 0, 32, [q]), (q, 1, 0, 32, [p]), (W[m][0], 0, 32, HALF, [q]), (W[m][1], 1, 32, HALF, [p]),
                                 (H[m][0], 2, 0, HALF, [H[m][1], p, q]), (H[m][1], 3, 0, HALF, [H[m][0], p, q])]:
            for t in ("sq", "ss"):
                call(c, ("sqd", 1), (t, HALF * b + lo, hi - lo, t, to, HALF * b + lo, on[c], "cst"))
    for h in range(2):
        w, r, z = W[R][h], H[R][h], HALF * h
        to = [W[k][h] for k in far[R]] + [W[peer[R]][h]]
        call(root, ("qb%d" % h, 1), ("bq", z, HALF, "bq", [w], z, on[root], "bc"))
        call(root, ("qb%d" % h, 1), ("bs", z, HALF, "bs", [r], z, on[root], "bp"))
        call(w, ("bc", None), ("bq", z, HALF, "bq", to, z, off[w], "bc"))
        call(r, ("bp", None), ("bs", z, HALF, "bs", to, z, off[r], "bp"))
    for h in range(2):
        z = HALF * h
        call(root, ("qb%d" % h, 1), ("bs", z, HALF, "bs", [W[R][h]], z, on[root], "bp"))
    for m in homes:
        for s, d in enumerate(dies):
            c = ranks[m][d]
            for t in "qs":
                call(c, ("qa", 4), ("a" + t, 0, 512, "w" + t, W[m], 512 * s, on[c], "w%d" % s))
    for m in homes:
        own = [ranks[m][d] for d in dies]
        cross = [ranks[far[m][0]][d] for d in dies]
        for h in range(2):
            w, r = W[m][h], H[m][h]
            for t in "qs":
                call(w, ("gqd", 1), ("g" + t, 0, HALF, "l" + t, [H[peer[m]][h]], HALF, off[w], "t1"),
                     ("g" + t, 0, HALF, "l" + t, [r], 0, near[w], "t0"))
            for t in "qs":
                call(r, ("gqd", 1), ("g" + t, 0, HALF, "c" + t, cross, 256 + HALF * h, off[r], "c1%d" % h),
                     ("g" + t, 0, HALF, "c" + t, own, HALF * h, near[r], "c0%d" % h))
    arrive = {}
    for c in range(WORLD):
        for _, tr in steps[c]:
            for t in tr:
                for k in t[4]:
                    arrive[(k, t[7])] = arrive.get((k, t[7]), 0) + ones(t[6])
    work = {c: h for m in homes for h, c in enumerate(W[m])}
    adds = [c for m in homes for c in H[m]]
    return steps, arrive, made, work, adds


def rank_program(g, core, T, topo):
    steps, arrive, made, work, adds = plan(T, topo)
    rank = T.rank_of(core)
    if not steps[core]:
        return
    sem = lambda name: T.sem[name]
    root = rank is not None and rank == T.root
    V, S, P, Y = g.vector, g.scalar, g.tensor, g.sync

    def arr(q, name):
        q.wait_ge(sem(name), arrive[(core, name)])

    def bank(j):
        return T.ps[:, 512 * j:512 * j + HALF]

    def unpack(j, b, q, s, z, start, stop):
        return P.matmul_mx(bank(j), T.sq[:, HALF * b:HALF * b + HALF], T.ss[:, HALF * b:HALF * b + HALF],
                           T[q][:, z:z + HALF], T[s][:, z:z + HALF], start, stop)

    if root:
        Y.dma_start(T.bt[:, 0:512], T.b[:, 0:512]).then_inc(sem("ldb0"), 16)
        S.dma_start(T.bt[:, 512:1024], T.b[:, 512:1024]).then_inc(sem("ldb1"), 16)
    if rank is not None:
        Y.dma_start(T.at[:], T.a[:]).then_inc(sem("lda"), 16)

    mine = made[core]
    V.memset(T.one[:], 1.0).then_inc(sem("mk"), 1)
    V.memset(T.sb[:, 0:512 * len(mine)], 0.0).then_inc(sem("mk"), 1)
    g.wait_ge(sem("mk"), 2)
    for j, b in enumerate(mine):
        g.affine_select(T.sb[:, 512 * j + b:512 * j + 512:4], T.one[:], [[-1, 128]], AluOpType.is_equal, 0.0, 0, 1).then_inc(sem("idt"), 1)
    for j, b in enumerate(mine):
        V.wait_ge(sem("idt"), j + 1)
        V.quantize_mx(T.sq[:, HALF * b:HALF * b + HALF], T.ss[:, HALF * b:HALF * b + HALF], T.sb[:, 512 * j:512 * j + 512]).then_inc(sem("sqd"), 1)

    sent = 0
    for (name, count), tr in steps[core]:
        g.wait_ge(sem(name), arrive[(core, name)] if count is None else count)
        ts = []
        for a, z0, n, b, to, z1, mask, s in tr:
            x, y = T[a][:, z0:z0 + n], T[b][:, z1:z1 + n]
            if a[-1] == "q":
                x, y = x.bitcast(dt.uint8), y.bitcast(dt.uint8)
            ids = []
            for d in to:
                rid, pid = topo.addr(d, core)
                ids.append(DstId(rid=rid, pnc=pid))
            ts.append(RemoteDMATransfer(dst_ids=ids, dma_engine_mask=mask, remote_sem=sem(s), srcs=[x], dsts=[y for _ in to]))
            sent += ones(mask)
        g.remote_dma_fused(ts, local_sem=sem("sent"))
    g.wait_ge(sem("sent"), sent)

    if core in work:
        z = HALF * work[core]
        for name in ("bc", "bp", "w0", "w1"):
            arr(P, name)
        for i in range(4):
            for s in range(2):
                c = 512 * s + HALF * i
                P.matmul_mx(bank(4 * s + i), T.wq[:, c:c + HALF], T.ws[:, c:c + HALF],
                            T.bq[:, z:z + HALF], T.bs[:, z:z + HALF], True, True).then_inc(sem("pm%d%d" % (s, i)), 1)
        for i in range(4):
            for s in range(2):
                out = (T.x0, T.x1)[s][:, i:512:4]
                onv = (s, i) == (1, 0)
                (V if onv else S).wait_ge(sem("pm%d%d" % (s, i)), 1)
                if onv:
                    V.tensor_scalar(out, bank(4 * s + i), 0.0, None, AluOpType.max).then_inc(sem("x%d" % i), 1)
                else:
                    S.activation(out, bank(4 * s + i), ActivationFunctionType.Relu).then_inc(sem("x%d" % i), 1)
            V.wait_ge(sem("x%d" % i), 2)
            V.tensor_tensor(T.gt[:, i:512:4], T.x0[:, i:512:4], T.x1[:, i:512:4], AluOpType.add).then_inc(sem("dn"), 1)

    if core in adds:
        P.wait_ge(sem("sqd"), len(mine))
        arr(P, "cst")
        for s in range(2):
            arr(P, "t%d" % s)
            for b in range(4):
                mm = unpack(b, b, "lq", "ls", HALF * s, s == 0, s == 1)
                if s == 1:
                    mm.then_inc(sem("gm%d" % b), 1)
        for b in range(4):
            if b % 2:
                V.wait_ge(sem("gm%d" % b), 1)
                V.tensor_copy(T.gt[:, b:512:4], bank(b)).then_inc(sem("dn"), 1)
            else:
                S.wait_ge(sem("gm%d" % b), 1)
                S.activation(T.gt[:, b:512:4], bank(b), ActivationFunctionType.Copy).then_inc(sem("dn"), 1)
    if core in work or core in adds:
        V.wait_ge(sem("dn"), 4)
        V.quantize_mx(T.gq[:], T.gs[:], T.gt[:]).then_inc(sem("gqd"), 1)
    if rank is None:
        return

    if root:
        for h in range(2):
            V.wait_ge(sem("ldb%d" % h), 16)
            V.quantize_mx(T.bq[:, HALF * h:HALF * h + HALF], T.bs[:, HALF * h:HALF * h + HALF], T.bt[:, 512 * h:512 * h + 512]).then_inc(sem("qb%d" % h), 1)
    V.wait_ge(sem("lda"), 16)
    for i in range(4):
        V.quantize_mx(T.aq[:, HALF * i:HALF * i + HALF], T["as"][:, HALF * i:HALF * i + HALF], T.at[:, 512 * i:512 * i + 512]).then_inc(sem("qa"), 1)

    P.wait_ge(sem("sqd"), len(mine))
    arr(P, "cst")
    for k in range(2):
        for h in range(2):
            arr(P, "c%d%d" % (k, h))
            for b in range(4):
                mm = unpack(4 * h + b, b, "cq", "cs", 256 * k + HALF * h, k == 0, k == 1)
                if k == 1:
                    mm.then_inc(sem("fm%d%d" % (h, b)), 1)
    for h in range(2):
        for b in range(4):
            out = T.ys[:, 512 * h + b:512 * h + 512:4]
            if b % 2:
                V.wait_ge(sem("fm%d%d" % (h, b)), 1)
                V.tensor_copy(out, bank(4 * h + b)).then_inc(sem("fe%d" % h), 1)
            else:
                S.wait_ge(sem("fm%d%d" % (h, b)), 1)
                S.activation(out, bank(4 * h + b), ActivationFunctionType.Copy).then_inc(sem("fe%d" % h), 1)
        Y.wait_ge(sem("fe%d" % h), 4)
        Y.dma_start(T.y[:, 512 * h:512 * h + 512], T.ys[:, 512 * h:512 * h + 512]).then_inc(sem("st%d" % h), 16)
    for h in range(2):
        Y.wait_ge(sem("st%d" % h), 16)
